import numpy as np
import ml_dtypes


def mxq(x, axis, fmt="e4m3"):
    dtype, down = {"e4m3": (ml_dtypes.float8_e4m3fn, 7), "e5m2": (ml_dtypes.float8_e5m2, 14)}[fmt]
    v = np.moveaxis(np.asarray(x, np.float32).astype(ml_dtypes.bfloat16).astype(np.float64), axis, -1)
    blocks = v.reshape(v.shape[:-1] + (-1, 32))
    amax = np.abs(blocks).max(-1, keepdims=True)
    byte = np.maximum(np.where(amax > 0, np.frexp(amax)[1] - 1 + 127, 0) - down, 1)
    scale = np.exp2(byte - 127.0)
    codes = (blocks / scale).astype(np.float32).astype(dtype).astype(np.float64)
    return np.moveaxis((codes * scale).reshape(v.shape), -1, axis)


WIDE = False


def mx_kscale(k):
    if not WIDE:
        return np.ones(k)
    levels = np.array([10, -10, 5, -5, 0])
    if k % 512:
        return np.exp2(np.random.permutation(np.resize(levels, k // 32))).repeat(32)
    a = np.empty((k // 512, 16))
    for p in range(k // 512):
        a[p, :8] = np.random.permutation(np.resize(levels, 8))
        for g in range(8):
            far = levels[np.abs(levels - a[p, g]) >= 10]
            a[p, g + 8] = far[np.random.randint(len(far))]
    return np.exp2(a.ravel()).repeat(32)


def f64(x):
    return np.asarray(x).astype(np.float64)


def striped(idx):
    return np.tile(idx.reshape(-1, 16).T, (8, 1)).astype(np.uint16)


def unstriped(offs):
    return offs[:16].T.reshape(-1).astype(np.int64)


def striped8(idx):
    return np.concatenate([x.reshape(-1, 16).T for x in idx]).astype(np.uint16)


def runs(offs, k):
    lists = np.stack([offs[16 * r : 16 * r + 16].T.reshape(-1) for r in range(8)]).astype(np.int64)
    return lists[np.arange(k) % 512 // 64]


def pack_weight(w):
    k, n = w.shape
    w = f64(np.asarray(w, np.float32).astype(ml_dtypes.bfloat16)).reshape(k // 32, 32, n)
    amax = np.abs(w).max(1)
    byte = np.clip(np.where(amax > 0, np.frexp(amax)[1] - 1 + 127 - 7, 1), 1, 254)
    scaled = (w * np.exp2(127.0 - byte)[:, None, :]).reshape(k, n).astype(np.float32)
    words = np.ascontiguousarray(scaled.reshape(k // 512, 128, 4, n).transpose(0, 1, 3, 2)).astype(ml_dtypes.float8_e4m3fn).view(np.uint8)
    return words, np.ascontiguousarray(byte.astype(np.uint8).reshape(k // 512, 16, n))


def unpack_weight(words, scales):
    g, p, n, _ = words.shape
    vals = np.ascontiguousarray(words).view(ml_dtypes.float8_e4m3fn).astype(np.float64) * np.repeat(np.exp2(scales.astype(np.float64) - 127.0), 8, axis=1)[..., None]
    return vals.transpose(0, 1, 3, 2).reshape(g * 512, n)


E2M1 = np.array([0.0, 0.5, 1.0, 1.5, 2.0, 3.0, 4.0, 6.0, -0.0, -0.5, -1.0, -1.5, -2.0, -3.0, -4.0, -6.0])


def pack_fp4(w):
    k, n = w.shape
    w = f64(np.asarray(w, np.float32).astype(ml_dtypes.bfloat16)).reshape(k // 32, 32, n)
    amax = np.abs(w).max(1)
    mant, ex = np.frexp(amax / 6.0)
    byte = np.clip(np.where(amax > 0, np.where(mant > 0.5, ex, ex - 1) + 127, 1), 1, 254)
    scaled = (w * np.exp2(127.0 - byte)[:, None, :]).reshape(k, n).astype(np.float32)
    c = np.ascontiguousarray(scaled.reshape(k // 512, 128, 4, n).transpose(0, 1, 3, 2)).astype(ml_dtypes.float4_e2m1fn).view(np.uint8) & 0xF
    words = (c[..., 0::2] | (c[..., 1::2] << 4)).reshape(k // 512, 128, 2 * n)
    return np.ascontiguousarray(words), np.ascontiguousarray(byte.astype(np.uint8).reshape(k // 512, 16, n))


def unpack_fp4(words, scales):
    g, _, n = scales.shape
    words = np.ascontiguousarray(words).reshape(g, 128, n, 2)
    nib = np.empty((g, 128, n, 4), np.uint8)
    nib[..., 0::2] = words & 0xF
    nib[..., 1::2] = words >> 4
    vals = E2M1[nib] * np.repeat(np.exp2(scales.astype(np.float64) - 127.0), 8, axis=1)[..., None]
    return vals.transpose(0, 1, 3, 2).reshape(g * 512, n)


def planes(y):
    n, m = y.shape
    v = y.astype(np.float32).astype(ml_dtypes.bfloat16).astype(np.float64).reshape(n // 32, 32, m)
    top = np.abs(v).max(1)
    byte = np.clip(np.where(top > 0, np.frexp(top)[1] - 1 + 127 - 7, 1), 1, 254)
    codes = (v * np.exp2(127.0 - byte)[:, None, :]).reshape(n, m).astype(np.float32).astype(ml_dtypes.float8_e4m3fn).view(np.uint8)
    words = codes.reshape(n // 512, 128, 4, m).transpose(0, 1, 3, 2)
    return np.ascontiguousarray(words), np.ascontiguousarray(byte.astype(np.uint8).reshape(n // 512, 16, m))


K, T, S, H, C = 512, 2048, 512, 512, 512


def setup_inputs():
    n = np.random.standard_normal
    s = mx_kscale(K)[:, None]
    packed_xT = pack_weight(n((K, T)) * s)
    packed_w1 = pack_fp4(n((K, H)) / np.sqrt(K) / s)
    return {
        "x_words": packed_xT[0],
        "x_scales": packed_xT[1],
        "w1_words": packed_w1[0],
        "w1_scales": packed_w1[1],
        "gs": (np.random.uniform(0.5, 1.5, (K, 1)) / s).astype(np.float32),
        "offs": striped(np.random.permutation(T)[:S]),
        "n1": striped8(np.stack([np.random.permutation(S) for _ in range(8)])),
        "n2": striped8(np.stack([np.random.permutation(S) for _ in range(8)])),
        "ca": striped(np.random.permutation(T)[:C]),
        "cb": striped(np.random.permutation(T)[:C]),
        "n3": striped8(np.stack([np.random.permutation(S) for _ in range(8)])),
        "n4": striped8(np.stack([np.random.permutation(S) for _ in range(8)])),
    }


def reference(x_words, x_scales, w1_words, w1_scales, gs, offs, n1, n2, ca, cb, n3, n4):
    x_ca = unpack_weight(x_words, x_scales)[:, unstriped(ca)]
    xq = unpack_weight(x_words, x_scales)[:, unstriped(offs)]
    y = unpack_fp4(w1_words, w1_scales).T @ xq
    pa = y[np.arange(H)[:, None], runs(n1, H)]
    pb = y[np.arange(H)[:, None], runs(n2, H)]
    z = f64(gs) * (np.maximum(np.minimum(y, pa), np.minimum(np.maximum(y, pa), pb)))
    zq = mxq(z, 0, "e4m3")
    a = 0.0625 * (x_ca.T @ zq)
    x_cb = unpack_weight(x_words, x_scales)[:, unstriped(cb)]
    b = 0.0625 * (x_cb.T @ zq)
    out_0 = 0.75 * (a * (b[np.arange(C)[:, None], runs(n4, C)]) - ((a[np.arange(C)[:, None], runs(n3, C)]) * b))
    return (out_0,) + planes(out_0)

@@ -1,0 +1,198 @@
+from contextlib import ExitStack
+
+import concourse.mybir as mybir
+
+F32 = mybir.dt.float32
+BF16 = mybir.dt.bfloat16
+I32 = mybir.dt.int32
+U32 = mybir.dt.uint32
+U16 = mybir.dt.uint16
+U8 = mybir.dt.uint8
+FP8X4 = mybir.dt.float8_e4m3fn_x4
+FP4X4 = mybir.dt.float4_e2m1fn_x4
+ALU = mybir.AluOpType
+COPY = mybir.ActivationFunctionType.Copy
+
+P = 128
+PACK = 4
+T = 2048
+S = 512
+FLOPS = 3 * 2 * 512 * 512 * 512
+
+Z_CHUNKS = ((0, 256), (256, 128), (384, 128))
+OUT_CHUNKS = ((0, 256), (256, 128), (384, 128))
+
+
+def tile_picked_ccmpcrossbmed_none_po_kernel(
+    tc, x_words, x_scales, w1_words, w1_scales, gs, offs, n1, n2, ca, cb, n3, n4, out_0, out_1, out_2
+):
+    nc = tc.nc
+    with ExitStack() as ctx:
+        keep = ctx.enter_context(tc.tile_pool(name="keep", bufs=1))
+        psum_y = ctx.enter_context(tc.psum_pool(name="psum_y", bufs=1))
+        psum_ab = ctx.enter_context(tc.psum_pool(name="psum_ab", bufs=4))
+
+        def load_list(name, source):
+            tile = keep.tile([P, S // 16], U16, name=name)
+            nc.sync.dma_start(tile[:], source)
+            return tile
+
+        def load_scale_rows(queue, tile, source):
+            for q in range(4):
+                queue.dma_start(
+                    tile[32 * q : 32 * q + 32, :].bitcast(I32),
+                    source[0, 4 * q : 4 * q + 4, :].bitcast(I32).partition_broadcast(8),
+                )
+
+        def entries(lst, start, width):
+            return lst[:, start // 16 : (start + width) // 16]
+
+        x_scale_table = keep.tile([P, T], U8, name="x_scale_table", align_bytes=64)
+        w_scale_raw = keep.tile([P, S], U8, name="w_scale_raw", tag="slot_b", align_bytes=64)
+
+        offs_sb = load_list("offs_sb", offs)
+        load_scale_rows(nc.sync, x_scale_table, x_scales)
+        ca_sb = load_list("ca_sb", ca)
+        w_word_raw = keep.tile([P, 2 * S], U8, name="w_word_raw", tag="slot_a", align_bytes=64)
+        nc.sync.dma_start(w_word_raw[:].bitcast(I32), w1_words[0].bitcast(I32))
+        x_word_table = keep.tile([P, T], I32, name="x_word_table", align_bytes=64)
+        nc.sync.dma_start(x_word_table[:], x_words[0].rearrange("p n r -> p (n r)").bitcast(I32))
+        load_scale_rows(nc.sync, w_scale_raw, w1_scales)
+        cb_sb = load_list("cb_sb", cb)
+        gain = keep.tile([P, PACK], F32, name="gain")
+        nc.sync.dma_start(gain[:], gs.rearrange("(p t) o -> p (t o)", t=PACK))
+        n1_sb = load_list("n1_sb", n1)
+        n4_sb = load_list("n4_sb", n4)
+        n2_sb = load_list("n2_sb", n2)
+        n3_sb = load_list("n3_sb", n3)
+
+        def gather_scales(name, lst):
+            tile = keep.tile([P, S], U8, name=name, align_bytes=64)
+            nc.vector.tensor_copy(tile[:], x_scale_table[:].indirect(lst[:]))
+            return tile
+
+        def gather_words(name, lst, tag):
+            tile = keep.tile([P, S], U32, name=name, tag=tag, align_bytes=64)
+            nc.vector.tensor_copy(tile[:], x_word_table[:].bitcast(U32).indirect(lst[:]))
+            return tile
+
+        def deal(name, source, dtype):
+            tile = keep.tile([P, S], dtype, name=name, align_bytes=64)
+            nc.vector.tensor_copy(
+                tile[:].rearrange("p (t m) -> p t m", t=PACK), source[:].rearrange("p (m t) -> p t m", t=PACK)
+            )
+            return tile
+
+        xq_scales = gather_scales("xq_scales", offs_sb)
+        xa_scales_raw = gather_scales("xa_scales_raw", ca_sb)
+        xb_scales_raw = gather_scales("xb_scales_raw", cb_sb)
+        w_words = keep.tile([P, 2 * S], U8, name="w_words", align_bytes=64)
+        nc.vector.tensor_copy(
+            w_words[:].rearrange("p (t m b) -> p t m b", t=PACK, b=2),
+            w_word_raw[:].rearrange("p (m t b) -> p t m b", t=PACK, b=2),
+        )
+        w_scales = deal("w_scales", w_scale_raw, U8)
+        xq_words = gather_words("xq_words", offs_sb, "xq_words")
+        xa_words_raw = gather_words("xa_words_raw", ca_sb, "slot_a")
+        xb_words_raw = gather_words("xb_words_raw", cb_sb, "slot_b")
+        xa_scales = deal("xa_scales", xa_scales_raw, U8)
+        xb_scales = deal("xb_scales", xb_scales_raw, U8)
+        xa_words = deal("xa_words", xa_words_raw, U32)
+        xb_words = deal("xb_words", xb_words_raw, U32)
+
+        y_banks = [psum_y.tile([P, S], F32, name="y_bank%d" % t) for t in range(PACK)]
+        y_rows = [keep.tile([P, S], F32, name="y_rows%d" % t) for t in range(PACK)]
+        y_bf = keep.tile([P, PACK, S], BF16, name="y_bf")
+        for t in range(PACK):
+            nc.tensor.matmul_mx(
+                out=y_banks[t][:],
+                lhsT=w_words[:, 2 * P * t : 2 * P * (t + 1)].bitcast(FP4X4),
+                lhsT_scale=w_scales[:, P * t : P * (t + 1)],
+                rhs=xq_words[:].bitcast(FP8X4),
+                rhs_scale=xq_scales[:],
+                start=True,
+                stop=True,
+            )
+        for t in range(PACK):
+            nc.scalar.activation(y_rows[t][:], y_banks[t][:], COPY, scale=gain[:, t : t + 1])
+        for t in range(PACK):
+            nc.scalar.activation(y_bf[:, t, :], y_banks[t][:], COPY, scale=gain[:, t : t + 1])
+
+        a_rows = [keep.tile([P, S], F32, name="a_rows%d" % t) for t in range(PACK)]
+        b_rows = [keep.tile([P, S], F32, name="b_rows%d" % t) for t in range(PACK)]
+
+        for c, (start, width) in enumerate(Z_CHUNKS):
+            cols = slice(start, start + width)
+            pa = keep.tile([P, PACK, width], BF16, name="pa%d" % c, tag="pa")
+            pb = keep.tile([P, PACK, width], BF16, name="pb%d" % c, tag="pb")
+            for t in range(PACK):
+                nc.vector.tensor_copy(pa[:, t, :], y_rows[t][:].indirect(entries(n1_sb, start, width)))
+                nc.vector.tensor_copy(pb[:, t, :], y_rows[t][:].indirect(entries(n2_sb, start, width)))
+            high = keep.tile([P, PACK, width], BF16, name="high%d" % c)
+            low = keep.tile([P, PACK, width], BF16, name="low%d" % c)
+            capped = keep.tile([P, PACK, width], BF16, name="capped%d" % c)
+            median = keep.tile([P, PACK, width], BF16, name="median%d" % c)
+            nc.vector.tensor_tensor(high[:], y_bf[:, :, cols], pa[:], ALU.max)
+            nc.vector.tensor_tensor(low[:], y_bf[:, :, cols], pa[:], ALU.min)
+            nc.vector.tensor_tensor(capped[:], high[:], pb[:], ALU.min)
+            nc.vector.tensor_tensor(median[:], low[:], capped[:], ALU.max)
+            z_grouped = keep.tile([P, width, PACK], BF16, name="z_grouped%d" % c, align_bytes=64)
+            if c == len(Z_CHUNKS) - 1:
+                nc.vector.tensor_copy(z_grouped[:], median[:].rearrange("p t j -> p j t"))
+            else:
+                nc.scalar.copy(z_grouped[:], median[:].rearrange("p t j -> p j t"))
+            z_words = keep.tile([P, width], U32, name="z_words%d" % c, align_bytes=64)
+            z_scales = keep.tile([P, width], U8, name="z_scales%d" % c, align_bytes=64)
+            nc.vector.quantize_mx(
+                out=z_words[:].bitcast(FP8X4), scales=z_scales[:], in_=z_grouped[:].rearrange("p j t -> p (j t)")
+            )
+            for t in range(PACK):
+                bank = psum_ab.tile([P, 2, 256], F32, name="ab_bank")
+                rows = slice(P * t, P * (t + 1))
+                for side, (words, scales) in enumerate(((xa_words, xa_scales), (xb_words, xb_scales))):
+                    nc.tensor.matmul_mx(
+                        out=bank[:, side, 0:width],
+                        lhsT=words[:, rows].bitcast(FP8X4),
+                        lhsT_scale=scales[:, rows],
+                        rhs=z_words[:].bitcast(FP8X4),
+                        rhs_scale=z_scales[:],
+                        start=True,
+                        stop=True,
+                    )
+                nc.scalar.activation(a_rows[t][:, cols], bank[:, 0, 0:width], COPY, scale=0.75 * 0.0625)
+                nc.scalar.activation(b_rows[t][:, cols], bank[:, 1, 0:width], COPY, scale=0.0625)
+
+        out_rows = out_0.rearrange("(p t) j -> p t j", t=PACK)
+        out_words_hbm = out_1[0].rearrange("p n r -> p (n r)").bitcast(I32)
+        out_scales = keep.tile([P, S], U8, name="out_scales", align_bytes=64)
+        for c, (start, width) in enumerate(OUT_CHUNKS):
+            cols = slice(start, start + width)
+            first = keep.tile([P, PACK, width], F32, name="first%d" % c, tag="first", bufs=2)
+            second = keep.tile([P, PACK, width], F32, name="second%d" % c, tag="second")
+            for t in range(PACK):
+                nc.vector.tensor_tensor(
+                    first[:, t, :], b_rows[t][:].indirect(entries(n4_sb, start, width)), a_rows[t][:, cols], ALU.mult
+                )
+                nc.vector.tensor_tensor(
+                    second[:, t, :], a_rows[t][:].indirect(entries(n3_sb, start, width)), b_rows[t][:, cols], ALU.mult
+                )
+            result = keep.tile([P, PACK, width], F32, name="result%d" % c)
+            nc.vector.tensor_tensor(result[:], first[:], second[:], ALU.subtract)
+            nc.sync.dma_start(out_rows[:, :, cols], result[:])
+            out_grouped = keep.tile([P, width, PACK], BF16, name="out_grouped%d" % c, align_bytes=64)
+            if c == len(OUT_CHUNKS) - 1:
+                nc.vector.tensor_copy(out_grouped[:], result[:].rearrange("p t j -> p j t"))
+            else:
+                nc.scalar.copy(out_grouped[:], result[:].rearrange("p t j -> p j t"))
+            out_words = keep.tile([P, width], I32, name="out_words%d" % c, align_bytes=64)
+            nc.vector.quantize_mx(
+                out=out_words[:].bitcast(FP8X4),
+                scales=out_scales[:, cols],
+                in_=out_grouped[:].rearrange("p j t -> p (j t)"),
+            )
+            nc.sync.dma_start(out_words_hbm[:, cols], out_words[:])
+        for q in range(4):
+            queue = nc.scalar if q % 2 else nc.sync
+            queue.dma_start(
+                out_2[0, 4 * q : 4 * q + 4, :].bitcast(I32), out_scales[32 * q : 32 * q + 4, :].bitcast(I32)
+            )

@@ -1,6 +1,7 @@
 from contextlib import ExitStack
 
 import concourse.mybir as mybir
+from concourse.masks import make_identity
 
 F32 = mybir.dt.float32
 BF16 = mybir.dt.bfloat16
@@ -19,8 +20,7 @@ T = 2048
 S = 512
 FLOPS = 3 * 2 * 512 * 512 * 512
 
-Z_CHUNKS = ((0, 256), (256, 128), (384, 128))
-OUT_CHUNKS = ((0, 256), (256, 128), (384, 128))
+HALF = S // 2
 
 
 def tile_picked_ccmpcrossbmed_none_po_kernel(
@@ -29,8 +29,10 @@ def tile_picked_ccmpcrossbmed_none_po_kernel(
     nc = tc.nc
     with ExitStack() as ctx:
         keep = ctx.enter_context(tc.tile_pool(name="keep", bufs=1))
-        psum_y = ctx.enter_context(tc.psum_pool(name="psum_y", bufs=1))
-        psum_ab = ctx.enter_context(tc.psum_pool(name="psum_ab", bufs=4))
+        psum_ring = ctx.enter_context(tc.psum_pool(name="psum_ring", bufs=4))
+        psum_late = ctx.enter_context(tc.psum_pool(name="psum_late", bufs=1))
+        identity = keep.tile([P, P], F32, name="identity")
+        make_identity(nc, identity[:])
 
         def load_list(name, source):
             tile = keep.tile([P, S // 16], U16, name=name)
@@ -50,11 +52,11 @@ def tile_picked_ccmpcrossbmed_none_po_kernel(
         x_scale_table = keep.tile([P, T], U8, name="x_scale_table", align_bytes=64)
         w_scale_raw = keep.tile([P, S], U8, name="w_scale_raw", tag="slot_b", align_bytes=64)
 
+        w_word_raw = keep.tile([P, 2 * S], U8, name="w_word_raw", tag="slot_a", align_bytes=64)
+        nc.sync.dma_start(w_word_raw[:].bitcast(I32), w1_words[0].bitcast(I32))
         offs_sb = load_list("offs_sb", offs)
         load_scale_rows(nc.sync, x_scale_table, x_scales)
         ca_sb = load_list("ca_sb", ca)
-        w_word_raw = keep.tile([P, 2 * S], U8, name="w_word_raw", tag="slot_a", align_bytes=64)
-        nc.sync.dma_start(w_word_raw[:].bitcast(I32), w1_words[0].bitcast(I32))
         x_word_table = keep.tile([P, T], I32, name="x_word_table", align_bytes=64)
         nc.sync.dma_start(x_word_table[:], x_words[0].rearrange("p n r -> p (n r)").bitcast(I32))
         load_scale_rows(nc.sync, w_scale_raw, w1_scales)
@@ -76,31 +78,38 @@ def tile_picked_ccmpcrossbmed_none_po_kernel(
             nc.vector.tensor_copy(tile[:], x_word_table[:].bitcast(U32).indirect(lst[:]))
             return tile
 
-        def deal(name, source, dtype):
+        def deal(name, source, dtype, run):
             tile = keep.tile([P, S], dtype, name=name, align_bytes=64)
             nc.vector.tensor_copy(
-                tile[:].rearrange("p (t m) -> p t m", t=PACK), source[:].rearrange("p (m t) -> p t m", t=PACK)
+                tile[:].rearrange("p (t c i) -> p c t i", t=PACK, i=run),
+                source[:].rearrange("p (c i t) -> p c t i", t=PACK, i=run),
             )
             return tile
+
+        def interleave(copy, grouped, planes):
+            copy(
+                grouped.rearrange("p (c i) t -> p c t i", i=4),
+                planes.rearrange("p t (c i) -> p c t i", i=4),
+            )
 
         xq_scales = gather_scales("xq_scales", offs_sb)
         xa_scales_raw = gather_scales("xa_scales_raw", ca_sb)
         xb_scales_raw = gather_scales("xb_scales_raw", cb_sb)
         w_words = keep.tile([P, 2 * S], U8, name="w_words", align_bytes=64)
         nc.vector.tensor_copy(
-            w_words[:].rearrange("p (t m b) -> p t m b", t=PACK, b=2),
-            w_word_raw[:].rearrange("p (m t b) -> p t m b", t=PACK, b=2),
+            w_words[:].rearrange("p (t c i b) -> p c t i b", t=PACK, i=8, b=2),
+            w_word_raw[:].rearrange("p (c i t b) -> p c t i b", t=PACK, i=8, b=2),
         )
-        w_scales = deal("w_scales", w_scale_raw, U8)
+        w_scales = deal("w_scales", w_scale_raw, U8, 16)
         xq_words = gather_words("xq_words", offs_sb, "xq_words")
         xa_words_raw = gather_words("xa_words_raw", ca_sb, "slot_a")
         xb_words_raw = gather_words("xb_words_raw", cb_sb, "slot_b")
-        xa_scales = deal("xa_scales", xa_scales_raw, U8)
-        xb_scales = deal("xb_scales", xb_scales_raw, U8)
-        xa_words = deal("xa_words", xa_words_raw, U32)
-        xb_words = deal("xb_words", xb_words_raw, U32)
+        xa_scales = deal("xa_scales", xa_scales_raw, U8, 16)
+        xb_scales = deal("xb_scales", xb_scales_raw, U8, 16)
+        xa_words = deal("xa_words", xa_words_raw, U32, 4)
+        xb_words = deal("xb_words", xb_words_raw, U32, 4)
 
-        y_banks = [psum_y.tile([P, S], F32, name="y_bank%d" % t) for t in range(PACK)]
+        y_banks = [psum_ring.tile([P, S], F32, name="y_bank%d" % t, tag="ring") for t in range(PACK)]
         y_rows = [keep.tile([P, S], F32, name="y_rows%d" % t) for t in range(PACK)]
         y_bf = keep.tile([P, PACK, S], BF16, name="y_bf")
         for t in range(PACK):
@@ -120,77 +129,134 @@ def tile_picked_ccmpcrossbmed_none_po_kernel(
 
         a_rows = [keep.tile([P, S], F32, name="a_rows%d" % t) for t in range(PACK)]
         b_rows = [keep.tile([P, S], F32, name="b_rows%d" % t) for t in range(PACK)]
+        b_negated = keep.tile([P, PACK, HALF], F32, name="b_negated", tag="negated")
 
-        for c, (start, width) in enumerate(Z_CHUNKS):
-            cols = slice(start, start + width)
-            pa = keep.tile([P, PACK, width], BF16, name="pa%d" % c, tag="pa")
-            pb = keep.tile([P, PACK, width], BF16, name="pb%d" % c, tag="pb")
+        banks = []
+        for half in range(2):
+            start = half * HALF
+            cols = slice(start, start + HALF)
+            pa = keep.tile([P, PACK, HALF], BF16, name="pa%d" % half, tag="pa")
+            pb = keep.tile([P, PACK, HALF], BF16, name="pb%d" % half, tag="pb", align_bytes=64)
             for t in range(PACK):
-                nc.vector.tensor_copy(pa[:, t, :], y_rows[t][:].indirect(entries(n1_sb, start, width)))
-                nc.vector.tensor_copy(pb[:, t, :], y_rows[t][:].indirect(entries(n2_sb, start, width)))
-            high = keep.tile([P, PACK, width], BF16, name="high%d" % c)
-            low = keep.tile([P, PACK, width], BF16, name="low%d" % c)
-            capped = keep.tile([P, PACK, width], BF16, name="capped%d" % c)
-            median = keep.tile([P, PACK, width], BF16, name="median%d" % c)
+                nc.vector.tensor_copy(pa[:, t, :], y_rows[t][:].indirect(entries(n1_sb, start, HALF)))
+            for t in range(PACK):
+                nc.vector.tensor_copy(pb[:, t, :], y_rows[t][:].indirect(entries(n2_sb, start, HALF)))
+            width = HALF if half == 0 else P
+            pieces = [slice(at, at + width) for at in range(0, HALF, width)]
+            high = keep.tile([P, PACK, HALF], BF16, name="high%d" % half)
+            low = keep.tile([P, PACK, HALF], BF16, name="low%d" % half)
+            capped = keep.tile([P, PACK, HALF], BF16, name="capped%d" % half)
+            median = keep.tile([P, PACK, HALF], BF16, name="median%d" % half)
             nc.vector.tensor_tensor(high[:], y_bf[:, :, cols], pa[:], ALU.max)
             nc.vector.tensor_tensor(low[:], y_bf[:, :, cols], pa[:], ALU.min)
-            nc.vector.tensor_tensor(capped[:], high[:], pb[:], ALU.min)
-            nc.vector.tensor_tensor(median[:], low[:], capped[:], ALU.max)
-            z_grouped = keep.tile([P, width, PACK], BF16, name="z_grouped%d" % c, align_bytes=64)
-            if c == len(Z_CHUNKS) - 1:
-                nc.vector.tensor_copy(z_grouped[:], median[:].rearrange("p t j -> p j t"))
+            for piece in pieces:
+                nc.vector.tensor_tensor(capped[:, :, piece], high[:, :, piece], pb[:, :, piece], ALU.min)
+            for piece in pieces:
+                nc.vector.tensor_tensor(median[:, :, piece], low[:, :, piece], capped[:, :, piece], ALU.max)
+            z_grouped = keep.tile([P, HALF, PACK], BF16, name="z_grouped%d" % half, tag="pb", align_bytes=64)
+            for piece in pieces:
+                interleave(
+                    nc.scalar.copy if piece.start == 0 else nc.vector.tensor_copy,
+                    z_grouped[:, piece, :],
+                    median[:, :, piece],
+                )
+            if half == 1:
+                for t in range(PACK):
+                    nc.scalar.activation(b_negated[:, t, :], banks[t][:, 0, :], COPY, scale=-0.0625)
+            z_words = keep.tile([P, HALF], U32, name="z_words%d" % half, align_bytes=64)
+            z_scales = keep.tile([P, HALF], U8, name="z_scales%d" % half, align_bytes=64)
+            for piece in pieces:
+                nc.vector.quantize_mx(
+                    out=z_words[:, piece].bitcast(FP8X4),
+                    scales=z_scales[:, piece],
+                    in_=z_grouped[:, piece, :].rearrange("p j t -> p (j t)"),
+                )
+            if half == 0:
+                banks = [psum_late.tile([P, 2, HALF], F32, name="ab_bank%d" % t, tag="late%d" % t) for t in range(PACK)]
             else:
-                nc.scalar.copy(z_grouped[:], median[:].rearrange("p t j -> p j t"))
-            z_words = keep.tile([P, width], U32, name="z_words%d" % c, align_bytes=64)
-            z_scales = keep.tile([P, width], U8, name="z_scales%d" % c, align_bytes=64)
-            nc.vector.quantize_mx(
-                out=z_words[:].bitcast(FP8X4), scales=z_scales[:], in_=z_grouped[:].rearrange("p j t -> p (j t)")
-            )
+                banks = [psum_ring.tile([P, 2, HALF], F32, name="ab_bank%d" % t, tag="ring") for t in range(PACK)]
             for t in range(PACK):
-                bank = psum_ab.tile([P, 2, 256], F32, name="ab_bank")
                 rows = slice(P * t, P * (t + 1))
-                for side, (words, scales) in enumerate(((xa_words, xa_scales), (xb_words, xb_scales))):
-                    nc.tensor.matmul_mx(
-                        out=bank[:, side, 0:width],
-                        lhsT=words[:, rows].bitcast(FP8X4),
-                        lhsT_scale=scales[:, rows],
-                        rhs=z_words[:].bitcast(FP8X4),
-                        rhs_scale=z_scales[:],
-                        start=True,
-                        stop=True,
-                    )
-                nc.scalar.activation(a_rows[t][:, cols], bank[:, 0, 0:width], COPY, scale=0.75 * 0.0625)
-                nc.scalar.activation(b_rows[t][:, cols], bank[:, 1, 0:width], COPY, scale=0.0625)
+                for piece in pieces if t == 0 else [slice(0, HALF)]:
+                    for side, (words, scales) in enumerate(((xb_words, xb_scales), (xa_words, xa_scales))):
+                        nc.tensor.matmul_mx(
+                            out=banks[t][:, side, piece],
+                            lhsT=words[:, rows].bitcast(FP8X4),
+                            lhsT_scale=scales[:, rows],
+                            rhs=z_words[:, piece].bitcast(FP8X4),
+                            rhs_scale=z_scales[:, piece],
+                            start=True,
+                            stop=True,
+                        )
+            for t in range(PACK):
+                nc.scalar.activation(b_rows[t][:, cols], banks[t][:, 0, :], COPY, scale=0.0625)
+                nc.scalar.activation(a_rows[t][:, cols], banks[t][:, 1, :], COPY, scale=0.75 * 0.0625)
 
         out_rows = out_0.rearrange("(p t) j -> p t j", t=PACK)
         out_words_hbm = out_1[0].rearrange("p n r -> p (n r)").bitcast(I32)
         out_scales = keep.tile([P, S], U8, name="out_scales", align_bytes=64)
-        for c, (start, width) in enumerate(OUT_CHUNKS):
-            cols = slice(start, start + width)
-            first = keep.tile([P, PACK, width], F32, name="first%d" % c, tag="first", bufs=2)
-            second = keep.tile([P, PACK, width], F32, name="second%d" % c, tag="second")
+
+        def quantize_out(name, grouped, cols, queue):
+            words = keep.tile([P, cols.stop - cols.start], I32, name=name, align_bytes=64)
+            nc.vector.quantize_mx(
+                out=words[:].bitcast(FP8X4), scales=out_scales[:, cols], in_=grouped.rearrange("p j t -> p (j t)")
+            )
+            queue.dma_start(out_words_hbm[:, cols], words[:])
+
+        def products(half):
+            start = half * HALF
+            cols = slice(start, start + HALF)
+            terms = keep.tile([P, 2, PACK, HALF], F32, name="terms%d" % half, tag="negated" if half else "terms")
+            first, second = terms[:, 0, :, :], terms[:, 1, :, :]
             for t in range(PACK):
                 nc.vector.tensor_tensor(
-                    first[:, t, :], b_rows[t][:].indirect(entries(n4_sb, start, width)), a_rows[t][:, cols], ALU.mult
+                    first[:, t, :], b_rows[t][:].indirect(entries(n4_sb, start, HALF)), a_rows[t][:, cols], ALU.mult
                 )
                 nc.vector.tensor_tensor(
-                    second[:, t, :], a_rows[t][:].indirect(entries(n3_sb, start, width)), b_rows[t][:, cols], ALU.mult
+                    second[:, t, :],
+                    a_rows[t][:].indirect(entries(n3_sb, start, HALF)),
+                    b_negated[:, t, :] if half == 0 else b_rows[t][:, cols],
+                    ALU.mult,
                 )
-            result = keep.tile([P, PACK, width], F32, name="result%d" % c)
-            nc.vector.tensor_tensor(result[:], first[:], second[:], ALU.subtract)
-            nc.sync.dma_start(out_rows[:, :, cols], result[:])
-            out_grouped = keep.tile([P, width, PACK], BF16, name="out_grouped%d" % c, align_bytes=64)
-            if c == len(OUT_CHUNKS) - 1:
-                nc.vector.tensor_copy(out_grouped[:], result[:].rearrange("p t j -> p j t"))
-            else:
-                nc.scalar.copy(out_grouped[:], result[:].rearrange("p t j -> p j t"))
-            out_words = keep.tile([P, width], I32, name="out_words%d" % c, align_bytes=64)
-            nc.vector.quantize_mx(
-                out=out_words[:].bitcast(FP8X4),
-                scales=out_scales[:, cols],
-                in_=out_grouped[:].rearrange("p j t -> p (j t)"),
-            )
-            nc.sync.dma_start(out_words_hbm[:, cols], out_words[:])
+            return first, second
+
+        blocks = [slice(at, at + P) for at in range(0, HALF, P)]
+        first, second = products(0)
+        turned_banks = [psum_late.tile([P, PACK, P], F32, name="turned_bank", tag="late%d" % n) for n in range(2)]
+        back_banks = [psum_late.tile([P, PACK, P], F32, name="back_bank", tag="late%d" % (2 + n)) for n in range(2)]
+        for t in range(PACK):
+            for bank, block in zip(turned_banks, blocks):
+                for term, opens in ((first, True), (second, False)):
+                    nc.tensor.matmul(
+                        bank[:, t, :], term[:, t, block], identity[:], start=opens, stop=not opens, is_transpose=True
+                    )
+        for n in range(2):
+            turned = keep.tile([P, PACK, P], F32, name="turned%d" % n)
+            nc.scalar.copy(turned[:], turned_banks[n][:])
+            for t in range(PACK):
+                nc.tensor.transpose(back_banks[n][:, t, :], turned[:, t, :], identity[:])
+        early_grouped = keep.tile([P, HALF, PACK], BF16, name="early_grouped", tag="early", align_bytes=64)
+        early_result = keep.tile([P, PACK, HALF], F32, name="early_result")
+        for bank, block in zip(back_banks, blocks):
+            interleave(nc.scalar.copy, early_grouped[:, block, :], bank[:])
+        for bank, block in zip(back_banks, blocks):
+            nc.scalar.copy(early_result[:, :, block], bank[:])
+        nc.scalar.dma_start(out_rows[:, :, 0:HALF], early_result[:])
+        quantize_out("early_words", early_grouped[:], slice(0, HALF), nc.scalar)
+
+        first, second = products(1)
+        late_result = keep.tile([P, PACK, HALF], F32, name="late_result")
+        most, last = slice(0, PACK - 1), slice(PACK - 1, PACK)
+        nc.vector.tensor_tensor(late_result[:, most, :], first[:, most, :], second[:, most, :], ALU.subtract)
+        nc.sync.dma_start(out_rows[:, most, HALF:S], late_result[:, most, :])
+        for block in blocks:
+            nc.vector.tensor_tensor(late_result[:, last, block], first[:, last, block], second[:, last, block], ALU.subtract)
+        nc.sync.dma_start(out_rows[:, last, HALF:S], late_result[:, last, :])
+        late_grouped = keep.tile([P, HALF, PACK], BF16, name="late_grouped", tag="early", align_bytes=64)
+        for block in blocks:
+            interleave(nc.vector.tensor_copy, late_grouped[:, block, :], late_result[:, :, block])
+        for n, block in enumerate(blocks):
+            quantize_out("late_words%d" % n, late_grouped[:, block, :], slice(HALF + block.start, HALF + block.stop), nc.sync)
         for q in range(4):
             queue = nc.scalar if q % 2 else nc.sync
             queue.dma_start(

@@ -31,8 +31,7 @@ def tile_picked_ccmpcrossbmed_none_po_kernel(
         keep = ctx.enter_context(tc.tile_pool(name="keep", bufs=1))
         psum_ring = ctx.enter_context(tc.psum_pool(name="psum_ring", bufs=4))
         psum_late = ctx.enter_context(tc.psum_pool(name="psum_late", bufs=1))
-        identity = keep.tile([P, P], F32, name="identity")
-        make_identity(nc, identity[:])
+
 
         def load_list(name, source):
             tile = keep.tile([P, S // 16], U16, name=name)
@@ -42,8 +41,8 @@ def tile_picked_ccmpcrossbmed_none_po_kernel(
         def load_scale_rows(queue, tile, source):
             for q in range(4):
                 queue.dma_start(
-                    tile[32 * q : 32 * q + 32, :].bitcast(I32),
-                    source[0, 4 * q : 4 * q + 4, :].bitcast(I32).partition_broadcast(8),
+                    tile[32 * q : 32 * q + 4, :].bitcast(I32),
+                    source[0, 4 * q : 4 * q + 4, :].bitcast(I32),
                 )
 
         def entries(lst, start, width):
@@ -51,6 +50,10 @@ def tile_picked_ccmpcrossbmed_none_po_kernel(
 
         x_scale_table = keep.tile([P, T], U8, name="x_scale_table", align_bytes=64)
         w_scale_raw = keep.tile([P, S], U8, name="w_scale_raw", tag="slot_b", align_bytes=64)
+        nc.gpsimd.memset(x_scale_table[:].bitcast(I32), 0)
+        nc.gpsimd.memset(w_scale_raw[:].bitcast(I32), 0)
+        identity = keep.tile([P, P], F32, name="identity")
+        make_identity(nc, identity[:])
 
         w_word_raw = keep.tile([P, 2 * S], U8, name="w_word_raw", tag="slot_a", align_bytes=64)
         nc.sync.dma_start(w_word_raw[:].bitcast(I32), w1_words[0].bitcast(I32))
@@ -203,7 +206,7 @@ def tile_picked_ccmpcrossbmed_none_po_kernel(
             )
             queue.dma_start(out_words_hbm[:, cols], words[:])
 
-        def products(half):
+        def products(half, result):
             start = half * HALF
             cols = slice(start, start + HALF)
             terms = keep.tile([P, 2, PACK, HALF], F32, name="terms%d" % half, tag="negated" if half else "terms")
@@ -212,6 +215,9 @@ def tile_picked_ccmpcrossbmed_none_po_kernel(
                 nc.vector.tensor_tensor(
                     first[:, t, :], b_rows[t][:].indirect(entries(n4_sb, start, HALF)), a_rows[t][:, cols], ALU.mult
                 )
+                if half == 1 and t == 2:
+                    nc.vector.tensor_tensor(result[:, 0:2, :], first[:, 0:2, :], second[:, 0:2, :], ALU.subtract)
+                    nc.sync.dma_start(out_rows[:, 0:2, cols], result[:, 0:2, :])
                 nc.vector.tensor_tensor(
                     second[:, t, :],
                     a_rows[t][:].indirect(entries(n3_sb, start, HALF)),
@@ -221,7 +227,7 @@ def tile_picked_ccmpcrossbmed_none_po_kernel(
             return first, second
 
         blocks = [slice(at, at + P) for at in range(0, HALF, P)]
-        first, second = products(0)
+        first, second = products(0, None)
         turned_banks = [psum_late.tile([P, PACK, P], F32, name="turned_bank", tag="late%d" % n) for n in range(2)]
         back_banks = [psum_late.tile([P, PACK, P], F32, name="back_bank", tag="late%d" % (2 + n)) for n in range(2)]
         for t in range(PACK):
@@ -242,16 +248,15 @@ def tile_picked_ccmpcrossbmed_none_po_kernel(
         for bank, block in zip(back_banks, blocks):
             nc.scalar.copy(early_result[:, :, block], bank[:])
         nc.scalar.dma_start(out_rows[:, :, 0:HALF], early_result[:])
-        quantize_out("early_words", early_grouped[:], slice(0, HALF), nc.scalar)
+        quantize_out("early_words", early_grouped[:], slice(0, HALF), nc.sync)
 
-        first, second = products(1)
         late_result = keep.tile([P, PACK, HALF], F32, name="late_result")
-        most, last = slice(0, PACK - 1), slice(PACK - 1, PACK)
+        first, second = products(1, late_result)
+        most, last = slice(2, 3), slice(3, 4)
         nc.vector.tensor_tensor(late_result[:, most, :], first[:, most, :], second[:, most, :], ALU.subtract)
-        nc.sync.dma_start(out_rows[:, most, HALF:S], late_result[:, most, :])
         for block in blocks:
             nc.vector.tensor_tensor(late_result[:, last, block], first[:, last, block], second[:, last, block], ALU.subtract)
-        nc.sync.dma_start(out_rows[:, last, HALF:S], late_result[:, last, :])
+        nc.sync.dma_start(out_rows[:, 2:4, HALF:S], late_result[:, 2:4, :])
         late_grouped = keep.tile([P, HALF, PACK], BF16, name="late_grouped", tag="early", align_bytes=64)
         for block in blocks:
             interleave(nc.vector.tensor_copy, late_grouped[:, block, :], late_result[:, :, block])

@@ -76,9 +76,10 @@ def tile_picked_ccmpcrossbmed_none_po_kernel(
             nc.vector.tensor_copy(tile[:], x_scale_table[:].indirect(lst[:]))
             return tile
 
-        def gather_words(name, lst, tag):
+        def gather_words(name, lst, tag, dealt):
             tile = keep.tile([P, S], U32, name=name, tag=tag, align_bytes=64)
-            nc.vector.tensor_copy(tile[:], x_word_table[:].bitcast(U32).indirect(lst[:]))
+            target = tile[:].rearrange("p (t m) -> p m t", t=PACK) if dealt else tile[:]
+            nc.vector.tensor_copy(target, x_word_table[:].bitcast(U32).indirect(lst[:]))
             return tile
 
         def deal(name, source, dtype, run):
@@ -104,13 +105,11 @@ def tile_picked_ccmpcrossbmed_none_po_kernel(
             w_word_raw[:].rearrange("p (c i t b) -> p c t i b", t=PACK, i=8, b=2),
         )
         w_scales = deal("w_scales", w_scale_raw, U8, 16)
-        xq_words = gather_words("xq_words", offs_sb, "xq_words")
-        xa_words_raw = gather_words("xa_words_raw", ca_sb, "slot_a")
-        xb_words_raw = gather_words("xb_words_raw", cb_sb, "slot_b")
+        xq_words = gather_words("xq_words", offs_sb, "xq_words", False)
+        xa_words = gather_words("xa_words", ca_sb, "slot_a", True)
+        xb_words = gather_words("xb_words", cb_sb, "slot_b", True)
         xa_scales = deal("xa_scales", xa_scales_raw, U8, 16)
         xb_scales = deal("xb_scales", xb_scales_raw, U8, 16)
-        xa_words = deal("xa_words", xa_words_raw, U32, 4)
-        xb_words = deal("xb_words", xb_words_raw, U32, 4)
 
         y_banks = [psum_ring.tile([P, S], F32, name="y_bank%d" % t, tag="ring") for t in range(PACK)]
         y_rows = [keep.tile([P, S], F32, name="y_rows%d" % t) for t in range(PACK)]
@@ -165,7 +164,7 @@ def tile_picked_ccmpcrossbmed_none_po_kernel(
                 )
             if half == 1:
                 for t in range(PACK):
-                    nc.scalar.activation(b_negated[:, t, :], banks[t][:, 0, :], COPY, scale=-0.0625)
+                    nc.scalar.activation(b_negated[:, t, :], banks[t % 2][:, t // 2, :], COPY, scale=-0.0625)
             z_words = keep.tile([P, HALF], U32, name="z_words%d" % half, align_bytes=64)
             z_scales = keep.tile([P, HALF], U8, name="z_scales%d" % half, align_bytes=64)
             for piece in pieces:
@@ -175,15 +174,18 @@ def tile_picked_ccmpcrossbmed_none_po_kernel(
                     in_=z_grouped[:, piece, :].rearrange("p j t -> p (j t)"),
                 )
             if half == 0:
-                banks = [psum_late.tile([P, 2, HALF], F32, name="ab_bank%d" % t, tag="late%d" % t) for t in range(PACK)]
+                banks = [psum_late.tile([P, 2, HALF], F32, name="ab_bank%d" % n, tag="late%d" % n) for n in range(PACK)]
             else:
-                banks = [psum_ring.tile([P, 2, HALF], F32, name="ab_bank%d" % t, tag="ring") for t in range(PACK)]
+                banks = [psum_ring.tile([P, 2, HALF], F32, name="ab_bank%d" % n, tag="ring") for n in range(PACK)]
             for t in range(PACK):
                 rows = slice(P * t, P * (t + 1))
-                for piece in pieces if t == 0 else [slice(0, HALF)]:
-                    for side, (words, scales) in enumerate(((xb_words, xb_scales), (xa_words, xa_scales))):
+                for side, (words, scales, window, factor) in enumerate(
+                    ((xb_words, xb_scales, b_rows[t], 0.0625), (xa_words, xa_scales, a_rows[t], 0.75 * 0.0625))
+                ):
+                    product = banks[2 * side + t % 2][:, t // 2, :]
+                    for piece in pieces if t == 0 else [slice(0, HALF)]:
                         nc.tensor.matmul_mx(
-                            out=banks[t][:, side, piece],
+                            out=product[:, piece],
                             lhsT=words[:, rows].bitcast(FP8X4),
                             lhsT_scale=scales[:, rows],
                             rhs=z_words[:, piece].bitcast(FP8X4),
@@ -191,9 +193,7 @@ def tile_picked_ccmpcrossbmed_none_po_kernel(
                             start=True,
                             stop=True,
                         )
-            for t in range(PACK):
-                nc.scalar.activation(b_rows[t][:, cols], banks[t][:, 0, :], COPY, scale=0.0625)
-                nc.scalar.activation(a_rows[t][:, cols], banks[t][:, 1, :], COPY, scale=0.75 * 0.0625)
+                    nc.scalar.activation(window[:, cols], product, COPY, scale=factor)
 
         out_rows = out_0.rearrange("(p t) j -> p t j", t=PACK)
         out_words_hbm = out_1[0].rearrange("p n r -> p (n r)").bitcast(I32)
@@ -244,10 +244,10 @@ def tile_picked_ccmpcrossbmed_none_po_kernel(
         early_grouped = keep.tile([P, HALF, PACK], BF16, name="early_grouped", tag="early", align_bytes=64)
         early_result = keep.tile([P, PACK, HALF], F32, name="early_result")
         for bank, block in zip(back_banks, blocks):
-            interleave(nc.scalar.copy, early_grouped[:, block, :], bank[:])
-        for bank, block in zip(back_banks, blocks):
             nc.scalar.copy(early_result[:, :, block], bank[:])
         nc.scalar.dma_start(out_rows[:, :, 0:HALF], early_result[:])
+        for block in blocks:
+            interleave(nc.scalar.copy, early_grouped[:, block, :], early_result[:, :, block])
         quantize_out("early_words", early_grouped[:], slice(0, HALF), nc.sync)
 
         late_result = keep.tile([P, PACK, HALF], F32, name="late_result")
@@ -260,8 +260,14 @@ def tile_picked_ccmpcrossbmed_none_po_kernel(
         late_grouped = keep.tile([P, HALF, PACK], BF16, name="late_grouped", tag="early", align_bytes=64)
         for block in blocks:
             interleave(nc.vector.tensor_copy, late_grouped[:, block, :], late_result[:, :, block])
-        for n, block in enumerate(blocks):
-            quantize_out("late_words%d" % n, late_grouped[:, block, :], slice(HALF + block.start, HALF + block.stop), nc.sync)
+        late_words = keep.tile([P, HALF], I32, name="late_words", align_bytes=64)
+        for block in blocks:
+            nc.vector.quantize_mx(
+                out=late_words[:, block].bitcast(FP8X4),
+                scales=out_scales[:, HALF + block.start : HALF + block.stop],
+                in_=late_grouped[:, block, :].rearrange("p j t -> p (j t)"),
+            )
+        nc.sync.dma_start(out_words_hbm[:, HALF:S], late_words[:])
         for q in range(4):
             queue = nc.scalar if q % 2 else nc.sync
             queue.dma_start(

from contextlib import ExitStack

import concourse.mybir as mybir
from concourse.masks import make_identity

F32 = mybir.dt.float32
BF16 = mybir.dt.bfloat16
I32 = mybir.dt.int32
U32 = mybir.dt.uint32
U16 = mybir.dt.uint16
U8 = mybir.dt.uint8
FP8X4 = mybir.dt.float8_e4m3fn_x4
FP4X4 = mybir.dt.float4_e2m1fn_x4
ALU = mybir.AluOpType
COPY = mybir.ActivationFunctionType.Copy

P = 128
PACK = 4
T = 2048
S = 512
FLOPS = 3 * 2 * 512 * 512 * 512

HALF = S // 2


def tile_picked_ccmpcrossbmed_none_po_kernel(
    tc, x_words, x_scales, w1_words, w1_scales, gs, offs, n1, n2, ca, cb, n3, n4, out_0, out_1, out_2
):
    nc = tc.nc
    with ExitStack() as ctx:
        keep = ctx.enter_context(tc.tile_pool(name="keep", bufs=1))
        psum_ring = ctx.enter_context(tc.psum_pool(name="psum_ring", bufs=4))
        psum_late = ctx.enter_context(tc.psum_pool(name="psum_late", bufs=1))


        def load_list(name, source):
            tile = keep.tile([P, S // 16], U16, name=name)
            nc.sync.dma_start(tile[:], source)
            return tile

        def load_scale_rows(queue, tile, source):
            for q in range(4):
                queue.dma_start(
                    tile[32 * q : 32 * q + 4, :].bitcast(I32),
                    source[0, 4 * q : 4 * q + 4, :].bitcast(I32),
                )

        def entries(lst, start, width):
            return lst[:, start // 16 : (start + width) // 16]

        x_scale_table = keep.tile([P, T], U8, name="x_scale_table", align_bytes=64)
        w_scale_raw = keep.tile([P, S], U8, name="w_scale_raw", tag="slot_b", align_bytes=64)
        nc.gpsimd.memset(x_scale_table[:].bitcast(I32), 0)
        nc.gpsimd.memset(w_scale_raw[:].bitcast(I32), 0)
        identity = keep.tile([P, P], F32, name="identity")
        make_identity(nc, identity[:])

        w_word_raw = keep.tile([P, 2 * S], U8, name="w_word_raw", tag="slot_a", align_bytes=64)
        nc.sync.dma_start(w_word_raw[:].bitcast(I32), w1_words[0].bitcast(I32))
        offs_sb = load_list("offs_sb", offs)
        load_scale_rows(nc.sync, x_scale_table, x_scales)
        ca_sb = load_list("ca_sb", ca)
        x_word_table = keep.tile([P, T], I32, name="x_word_table", align_bytes=64)
        nc.sync.dma_start(x_word_table[:], x_words[0].rearrange("p n r -> p (n r)").bitcast(I32))
        load_scale_rows(nc.sync, w_scale_raw, w1_scales)
        cb_sb = load_list("cb_sb", cb)
        gain = keep.tile([P, PACK], F32, name="gain")
        nc.sync.dma_start(gain[:], gs.rearrange("(p t) o -> p (t o)", t=PACK))
        n1_sb = load_list("n1_sb", n1)
        n4_sb = load_list("n4_sb", n4)
        n2_sb = load_list("n2_sb", n2)
        n3_sb = load_list("n3_sb", n3)

        def gather_scales(name, lst):
            tile = keep.tile([P, S], U8, name=name, align_bytes=64)
            nc.vector.tensor_copy(tile[:], x_scale_table[:].indirect(lst[:]))
            return tile

        def gather_words(name, lst, tag, dealt):
            tile = keep.tile([P, S], U32, name=name, tag=tag, align_bytes=64)
            target = tile[:].rearrange("p (t m) -> p m t", t=PACK) if dealt else tile[:]
            nc.vector.tensor_copy(target, x_word_table[:].bitcast(U32).indirect(lst[:]))
            return tile

        def deal(name, source, dtype, run):
            tile = keep.tile([P, S], dtype, name=name, align_bytes=64)
            nc.vector.tensor_copy(
                tile[:].rearrange("p (t c i) -> p c t i", t=PACK, i=run),
                source[:].rearrange("p (c i t) -> p c t i", t=PACK, i=run),
            )
            return tile

        def interleave(copy, grouped, planes):
            copy(
                grouped.rearrange("p (c i) t -> p c t i", i=4),
                planes.rearrange("p t (c i) -> p c t i", i=4),
            )

        xq_scales = gather_scales("xq_scales", offs_sb)
        xa_scales_raw = gather_scales("xa_scales_raw", ca_sb)
        xb_scales_raw = gather_scales("xb_scales_raw", cb_sb)
        w_words = keep.tile([P, 2 * S], U8, name="w_words", align_bytes=64)
        nc.vector.tensor_copy(
            w_words[:].rearrange("p (t c i b) -> p c t i b", t=PACK, i=8, b=2),
            w_word_raw[:].rearrange("p (c i t b) -> p c t i b", t=PACK, i=8, b=2),
        )
        w_scales = deal("w_scales", w_scale_raw, U8, 16)
        xq_words = gather_words("xq_words", offs_sb, "xq_words", False)
        xa_words = gather_words("xa_words", ca_sb, "slot_a", True)
        xb_words = gather_words("xb_words", cb_sb, "slot_b", True)
        xa_scales = deal("xa_scales", xa_scales_raw, U8, 16)
        xb_scales = deal("xb_scales", xb_scales_raw, U8, 16)

        y_banks = [psum_ring.tile([P, S], F32, name="y_bank%d" % t, tag="ring") for t in range(PACK)]
        y_rows = [keep.tile([P, S], F32, name="y_rows%d" % t) for t in range(PACK)]
        y_bf = keep.tile([P, PACK, S], BF16, name="y_bf")
        for t in range(PACK):
            nc.tensor.matmul_mx(
                out=y_banks[t][:],
                lhsT=w_words[:, 2 * P * t : 2 * P * (t + 1)].bitcast(FP4X4),
                lhsT_scale=w_scales[:, P * t : P * (t + 1)],
                rhs=xq_words[:].bitcast(FP8X4),
                rhs_scale=xq_scales[:],
                start=True,
                stop=True,
            )
        for t in range(PACK):
            nc.scalar.activation(y_rows[t][:], y_banks[t][:], COPY, scale=gain[:, t : t + 1])
        for t in range(PACK):
            nc.scalar.activation(y_bf[:, t, :], y_banks[t][:], COPY, scale=gain[:, t : t + 1])

        a_rows = [keep.tile([P, S], F32, name="a_rows%d" % t) for t in range(PACK)]
        b_rows = [keep.tile([P, S], F32, name="b_rows%d" % t) for t in range(PACK)]
        b_negated = keep.tile([P, PACK, HALF], F32, name="b_negated", tag="negated")

        banks = []
        for half in range(2):
            start = half * HALF
            cols = slice(start, start + HALF)
            pa = keep.tile([P, PACK, HALF], BF16, name="pa%d" % half, tag="pa")
            pb = keep.tile([P, PACK, HALF], BF16, name="pb%d" % half, tag="pb", align_bytes=64)
            for t in range(PACK):
                nc.vector.tensor_copy(pa[:, t, :], y_rows[t][:].indirect(entries(n1_sb, start, HALF)))
            for t in range(PACK):
                nc.vector.tensor_copy(pb[:, t, :], y_rows[t][:].indirect(entries(n2_sb, start, HALF)))
            width = HALF if half == 0 else P
            pieces = [slice(at, at + width) for at in range(0, HALF, width)]
            high = keep.tile([P, PACK, HALF], BF16, name="high%d" % half)
            low = keep.tile([P, PACK, HALF], BF16, name="low%d" % half)
            capped = keep.tile([P, PACK, HALF], BF16, name="capped%d" % half)
            median = keep.tile([P, PACK, HALF], BF16, name="median%d" % half)
            nc.vector.tensor_tensor(high[:], y_bf[:, :, cols], pa[:], ALU.max)
            nc.vector.tensor_tensor(low[:], y_bf[:, :, cols], pa[:], ALU.min)
            for piece in pieces:
                nc.vector.tensor_tensor(capped[:, :, piece], high[:, :, piece], pb[:, :, piece], ALU.min)
            for piece in pieces:
                nc.vector.tensor_tensor(median[:, :, piece], low[:, :, piece], capped[:, :, piece], ALU.max)
            z_grouped = keep.tile([P, HALF, PACK], BF16, name="z_grouped%d" % half, tag="pb", align_bytes=64)
            for piece in pieces:
                interleave(
                    nc.scalar.copy if piece.start == 0 else nc.vector.tensor_copy,
                    z_grouped[:, piece, :],
                    median[:, :, piece],
                )
            if half == 1:
                for t in range(PACK):
                    nc.scalar.activation(b_negated[:, t, :], banks[t % 2][:, t // 2, :], COPY, scale=-0.0625)
            z_words = keep.tile([P, HALF], U32, name="z_words%d" % half, align_bytes=64)
            z_scales = keep.tile([P, HALF], U8, name="z_scales%d" % half, align_bytes=64)
            for piece in pieces:
                nc.vector.quantize_mx(
                    out=z_words[:, piece].bitcast(FP8X4),
                    scales=z_scales[:, piece],
                    in_=z_grouped[:, piece, :].rearrange("p j t -> p (j t)"),
                )
            if half == 0:
                banks = [psum_late.tile([P, 2, HALF], F32, name="ab_bank%d" % n, tag="late%d" % n) for n in range(PACK)]
            else:
                banks = [psum_ring.tile([P, 2, HALF], F32, name="ab_bank%d" % n, tag="ring") for n in range(PACK)]
            for t in range(PACK):
                rows = slice(P * t, P * (t + 1))
                for side, (words, scales, window, factor) in enumerate(
                    ((xb_words, xb_scales, b_rows[t], 0.0625), (xa_words, xa_scales, a_rows[t], 0.75 * 0.0625))
                ):
                    product = banks[2 * side + t % 2][:, t // 2, :]
                    for piece in pieces if t == 0 else [slice(0, HALF)]:
                        nc.tensor.matmul_mx(
                            out=product[:, piece],
                            lhsT=words[:, rows].bitcast(FP8X4),
                            lhsT_scale=scales[:, rows],
                            rhs=z_words[:, piece].bitcast(FP8X4),
                            rhs_scale=z_scales[:, piece],
                            start=True,
                            stop=True,
                        )
                    nc.scalar.activation(window[:, cols], product, COPY, scale=factor)

        out_rows = out_0.rearrange("(p t) j -> p t j", t=PACK)
        out_words_hbm = out_1[0].rearrange("p n r -> p (n r)").bitcast(I32)
        out_scales = keep.tile([P, S], U8, name="out_scales", align_bytes=64)

        def quantize_out(name, grouped, cols, queue):
            words = keep.tile([P, cols.stop - cols.start], I32, name=name, align_bytes=64)
            nc.vector.quantize_mx(
                out=words[:].bitcast(FP8X4), scales=out_scales[:, cols], in_=grouped.rearrange("p j t -> p (j t)")
            )
            queue.dma_start(out_words_hbm[:, cols], words[:])

        def products(half, result):
            start = half * HALF
            cols = slice(start, start + HALF)
            terms = keep.tile([P, 2, PACK, HALF], F32, name="terms%d" % half, tag="negated" if half else "terms")
            first, second = terms[:, 0, :, :], terms[:, 1, :, :]
            for t in range(PACK):
                nc.vector.tensor_tensor(
                    first[:, t, :], b_rows[t][:].indirect(entries(n4_sb, start, HALF)), a_rows[t][:, cols], ALU.mult
                )
                if half == 1 and t == 2:
                    nc.vector.tensor_tensor(result[:, 0:2, :], first[:, 0:2, :], second[:, 0:2, :], ALU.subtract)
                    nc.sync.dma_start(out_rows[:, 0:2, cols], result[:, 0:2, :])
                nc.vector.tensor_tensor(
                    second[:, t, :],
                    a_rows[t][:].indirect(entries(n3_sb, start, HALF)),
                    b_negated[:, t, :] if half == 0 else b_rows[t][:, cols],
                    ALU.mult,
                )
            return first, second

        blocks = [slice(at, at + P) for at in range(0, HALF, P)]
        first, second = products(0, None)
        turned_banks = [psum_late.tile([P, PACK, P], F32, name="turned_bank", tag="late%d" % n) for n in range(2)]
        back_banks = [psum_late.tile([P, PACK, P], F32, name="back_bank", tag="late%d" % (2 + n)) for n in range(2)]
        for t in range(PACK):
            for bank, block in zip(turned_banks, blocks):
                for term, opens in ((first, True), (second, False)):
                    nc.tensor.matmul(
                        bank[:, t, :], term[:, t, block], identity[:], start=opens, stop=not opens, is_transpose=True
                    )
        for n in range(2):
            turned = keep.tile([P, PACK, P], F32, name="turned%d" % n)
            nc.scalar.copy(turned[:], turned_banks[n][:])
            for t in range(PACK):
                nc.tensor.transpose(back_banks[n][:, t, :], turned[:, t, :], identity[:])
        early_grouped = keep.tile([P, HALF, PACK], BF16, name="early_grouped", tag="early", align_bytes=64)
        early_result = keep.tile([P, PACK, HALF], F32, name="early_result")
        for bank, block in zip(back_banks, blocks):
            nc.scalar.copy(early_result[:, :, block], bank[:])
        nc.scalar.dma_start(out_rows[:, :, 0:HALF], early_result[:])
        for block in blocks:
            interleave(nc.scalar.copy, early_grouped[:, block, :], early_result[:, :, block])
        quantize_out("early_words", early_grouped[:], slice(0, HALF), nc.sync)

        late_result = keep.tile([P, PACK, HALF], F32, name="late_result")
        first, second = products(1, late_result)
        most, last = slice(2, 3), slice(3, 4)
        nc.vector.tensor_tensor(late_result[:, most, :], first[:, most, :], second[:, most, :], ALU.subtract)
        for block in blocks:
            nc.vector.tensor_tensor(late_result[:, last, block], first[:, last, block], second[:, last, block], ALU.subtract)
        nc.sync.dma_start(out_rows[:, 2:4, HALF:S], late_result[:, 2:4, :])
        late_grouped = keep.tile([P, HALF, PACK], BF16, name="late_grouped", tag="early", align_bytes=64)
        for block in blocks:
            interleave(nc.vector.tensor_copy, late_grouped[:, block, :], late_result[:, :, block])
        late_words = keep.tile([P, HALF], I32, name="late_words", align_bytes=64)
        for block in blocks:
            nc.vector.quantize_mx(
                out=late_words[:, block].bitcast(FP8X4),
                scales=out_scales[:, HALF + block.start : HALF + block.stop],
                in_=late_grouped[:, block, :].rearrange("p j t -> p (j t)"),
            )
        nc.sync.dma_start(out_words_hbm[:, HALF:S], late_words[:])
        for q in range(4):
            queue = nc.scalar if q % 2 else nc.sync
            queue.dma_start(
                out_2[0, 4 * q : 4 * q + 4, :].bitcast(I32), out_scales[32 * q : 32 * q + 4, :].bitcast(I32)
            )
